import numpy as np
import ml_dtypes


def mxq(x, axis, fmt="e4m3"):
    dtype, down = {"e4m3": (ml_dtypes.float8_e4m3fn, 7), "e5m2": (ml_dtypes.float8_e5m2, 14)}[fmt]
    v = np.moveaxis(np.asarray(x, np.float32).astype(ml_dtypes.bfloat16).astype(np.float64), axis, -1)
    blocks = v.reshape(v.shape[:-1] + (-1, 32))
    amax = np.abs(blocks).max(-1, keepdims=True)
    byte = np.maximum(np.where(amax > 0, np.frexp(amax)[1] - 1 + 127, 0) - down, 1)
    scale = np.exp2(byte - 127.0)
    codes = (blocks / scale).astype(np.float32).astype(dtype).astype(np.float64)
    return np.moveaxis((codes * scale).reshape(v.shape), -1, axis)


WIDE = False


def mx_kscale(k):
    if not WIDE:
        return np.ones(k)
    levels = np.array([10, -10, 5, -5, 0])
    if k % 512:
        return np.exp2(np.random.permutation(np.resize(levels, k // 32))).repeat(32)
    a = np.empty((k // 512, 16))
    for p in range(k // 512):
        a[p, :8] = np.random.permutation(np.resize(levels, 8))
        for g in range(8):
            far = levels[np.abs(levels - a[p, g]) >= 10]
            a[p, g + 8] = far[np.random.randint(len(far))]
    return np.exp2(a.ravel()).repeat(32)


BF16 = ml_dtypes.bfloat16


def bf(x):
    return np.asarray(x, np.float32).astype(BF16)


def f64(x):
    return np.asarray(x).astype(np.float64)


E2M1 = np.array([0.0, 0.5, 1.0, 1.5, 2.0, 3.0, 4.0, 6.0, -0.0, -0.5, -1.0, -1.5, -2.0, -3.0, -4.0, -6.0])


def pack_weight(w, fmt):
    k, n = w.shape
    w = f64(bf(w)).reshape(k // 32, 32, n)
    amax = np.abs(w).max(1)
    if fmt == "e4m3":
        byte = np.frexp(amax)[1] - 1 + 127 - 7
    else:
        mant, ex = np.frexp(amax / 6.0)
        byte = np.where(mant > 0.5, ex, ex - 1) + 127
    byte = np.clip(np.where(amax > 0, byte, 1), 1, 254)
    scaled = (w * np.exp2(127.0 - byte)[:, None, :]).reshape(k, n).astype(np.float32)
    by_word = np.ascontiguousarray(scaled.reshape(k // 512, 128, 4, n).transpose(0, 1, 3, 2))
    if fmt == "e4m3":
        words = by_word.astype(ml_dtypes.float8_e4m3fn).view(np.uint8)
    else:
        c = by_word.astype(ml_dtypes.float4_e2m1fn).view(np.uint8) & 0xF
        words = c[..., 0::2] | (c[..., 1::2] << 4)
    return np.ascontiguousarray(words), np.ascontiguousarray(byte.astype(np.uint8).reshape(k // 512, 16, n))


def unpack_weight(words, scales, fmt):
    g, p, n, _ = words.shape
    if fmt == "e4m3":
        vals = np.ascontiguousarray(words).view(ml_dtypes.float8_e4m3fn).astype(np.float64)
    else:
        nib = np.empty((g, p, n, 4), np.uint8)
        nib[..., 0::2] = words & 0xF
        nib[..., 1::2] = words >> 4
        vals = E2M1[nib]
    vals = vals * np.repeat(np.exp2(scales.astype(np.float64) - 127.0), 8, axis=1)[..., None]
    return vals.transpose(0, 1, 3, 2).reshape(g * 512, n)


T, N, R, O = 1024, 1024, 512, 512


def draw0():
    s, t = mx_kscale(N), mx_kscale(R)
    x = bf(np.random.standard_normal((T, N)) * s)
    a_words, a_scales = pack_weight(np.random.standard_normal((N, R)) / np.sqrt(N) / s[:, None], "e4m3")
    b_words, b_scales = pack_weight(np.random.standard_normal((N, R)) / np.sqrt(N) / s[:, None] * t, "e4m3")
    h1_words, h1_scales = pack_weight(np.random.standard_normal((N, O)) / np.sqrt(N) / s[:, None], "e4m3")
    h2_words, h2_scales = pack_weight(np.random.standard_normal((R, O)) / np.sqrt(R) / t[:, None], "e4m3")
    h3_words, h3_scales = pack_weight(0.5 * np.random.standard_normal((R, O)) / np.sqrt(R) / t[:, None], "e4m3")
    return {
        "x": x,
        "a_words": a_words,
        "a_scales": a_scales,
        "b_words": b_words,
        "b_scales": b_scales,
        "h1_words": h1_words,
        "h1_scales": h1_scales,
        "h2_words": h2_words,
        "h2_scales": h2_scales,
        "h3_words": h3_words,
        "h3_scales": h3_scales,
    }


def core(x, a_words, a_scales, b_words, b_scales, h1_words, h1_scales, h2_words, h2_scales, h3_words, h3_scales):
    xq = mxq(f64(x), 1, "e4m3")
    p = xq @ unpack_weight(a_words, a_scales, "e4m3")
    q = xq @ unpack_weight(b_words, b_scales, "e4m3")
    k2 = p * q
    k3 = p * k2
    y1 = xq @ unpack_weight(h1_words, h1_scales, "e4m3")
    y2 = mxq(k2, 1, "e4m3") @ unpack_weight(h2_words, h2_scales, "e4m3")
    y3 = mxq(k3, 1, "e4m3") @ unpack_weight(h3_words, h3_scales, "e4m3")
    return y1 + y2 + y3


def e4m3fn_bytes(y):
    return np.clip(np.asarray(y, np.float64), -448.0, 448.0).astype(np.float32).astype(ml_dtypes.float8_e4m3fn).view(np.uint8)


def e4m3fn_values(b):
    return np.asarray(b, np.uint8).view(ml_dtypes.float8_e4m3fn).astype(np.float64)


def setup_inputs():
    d = draw0()
    x0 = np.asarray(d['x']).astype(np.float64)
    s = (np.max(np.abs(x0), axis=(0,), keepdims=True) / 448.0).astype(np.float32)
    out = {}
    for k, v in d.items():
        if k == 'x':
            out['x_bytes'] = e4m3fn_bytes(x0 / s.astype(np.float64))
            out['x_scale'] = s
        else:
            out[k] = v
    return out


def reference(x_bytes, x_scale, a_words, a_scales, b_words, b_scales, h1_words, h1_scales, h2_words, h2_scales, h3_words, h3_scales):
    return core(e4m3fn_values(x_bytes) * x_scale.astype(np.float64), a_words, a_scales, b_words, b_scales, h1_words, h1_scales, h2_words, h2_scales, h3_words, h3_scales)

@@ -1,0 +1,253 @@
+from contextlib import ExitStack
+
+import concourse.mybir as mybir
+from concourse.masks import make_identity
+
+T, N, R, O = 1024, 1024, 512, 512
+FLOPS = 2 * T * (2 * N * R + N * O + 2 * R * O)
+
+F32 = mybir.dt.float32
+BF16 = mybir.dt.bfloat16
+I32 = mybir.dt.int32
+U8 = mybir.dt.uint8
+FP8 = mybir.dt.float8_e4m3fn
+FP8X4 = mybir.dt.float8_e4m3fn_x4
+MULT = mybir.AluOpType.mult
+
+P = 128
+PACK = 4
+G = N // (P * PACK)
+TILES = T // P
+QUADS = 4
+ROWS = 4
+
+
+def tile_factoredcubicvolterraequalizer_w8_kernel(
+    tc, x_bytes, x_scale, a_words, a_scales, b_words, b_scales, h1_words, h1_scales,
+    h2_words, h2_scales, h3_words, h3_scales, out
+):
+    nc = tc.nc
+    with ExitStack() as ctx:
+        keep = ctx.enter_context(tc.tile_pool(name="keep", bufs=1))
+        work = ctx.enter_context(tc.tile_pool(name="work", bufs=3))
+        psum = ctx.enter_context(tc.psum_pool(name="psum", bufs=2))
+        ctx.enter_context(tc.manual_schedule())
+
+        ident = keep.tile([P, P], F32, name="ident")
+        make_identity(nc, ident[:])
+
+        def words_view(words):
+            return words.rearrange("g p n t -> p g (n t)").bitcast(I32)
+
+        def load_scales(plane, first_row, scales, queue):
+            groups = scales.shape[0]
+            for quad in range(QUADS):
+                lo = 32 * quad + first_row
+                queue.dma_start(
+                    out=plane[lo : lo + ROWS * groups, :].bitcast(I32),
+                    in_=scales[:, ROWS * quad : ROWS * (quad + 1), :].bitcast(I32),
+                )
+
+        b_sc_raw = keep.tile([P, R], U8, name="b_sc_raw", align_bytes=64)
+        a_sc_raw = keep.tile([P, R], U8, name="a_sc_raw", align_bytes=64)
+        h_sc = keep.tile([P, O], U8, name="h_sc", align_bytes=64)
+        for plane in (a_sc_raw, b_sc_raw, h_sc):
+            nc.vector.memset(plane[:].bitcast(I32), 0)
+
+        x_raw = {}
+
+        def load_x(first, count):
+            xbytes = keep.tile([P, count, N], U8, name="xbytes%d" % first, align_bytes=64)
+            rows = x_bytes[first * P : (first + count) * P, :]
+            nc.sync.dma_start(out=xbytes[:], in_=rows.rearrange("(j p) k -> p j k", p=P))
+            for j in range(count):
+                x_raw[first + j] = xbytes[:, j, :]
+
+        x_sc = keep.tile([P, G, PACK], F32, name="x_sc")
+        b_raw = keep.tile([P, G, R], I32, name="b_raw", align_bytes=64)
+        a_raw = keep.tile([P, G, R], I32, name="a_raw", align_bytes=64)
+        h1_w = keep.tile([P, G, O], I32, name="h1_w", align_bytes=64)
+        h2_w = keep.tile([P, 1, O], I32, name="h2_w", align_bytes=64)
+        h3_w = keep.tile([P, 1, O], I32, name="h3_w", align_bytes=64)
+
+        load_x(0, 1)
+        nc.sync.dma_start(out=x_sc[:], in_=x_scale.rearrange("o (g p t) -> p (o g) t", p=P, t=PACK))
+        load_scales(a_sc_raw, 0, a_scales, nc.sync)
+        nc.sync.dma_start(out=a_raw[:], in_=words_view(a_words))
+        load_x(1, 1)
+        load_scales(b_sc_raw, 0, b_scales, nc.sync)
+        nc.sync.dma_start(out=b_raw[:], in_=words_view(b_words))
+        load_x(2, 2)
+        load_scales(h_sc, 0, h1_scales, nc.sync)
+        load_scales(h_sc, 8, h2_scales, nc.sync)
+        load_scales(h_sc, 12, h3_scales, nc.sync)
+        nc.sync.dma_start(out=h1_w[:], in_=words_view(h1_words))
+        nc.sync.dma_start(out=h2_w[:], in_=words_view(h2_words))
+        nc.sync.dma_start(out=h3_w[:], in_=words_view(h3_words))
+        load_x(4, 4)
+
+        def permute(name, raw, sc_raw):
+            w = keep.tile([P, G, R], I32, name=name + "_w", align_bytes=64)
+            sc = keep.tile([P, R], U8, name=name + "_sc", align_bytes=64)
+            nc.vector.tensor_copy(
+                out=sc[:].rearrange("p (t m) -> p t m", t=PACK),
+                in_=sc_raw[:].rearrange("p (m t) -> p t m", t=PACK),
+            )
+            nc.vector.tensor_copy(
+                out=w[:].rearrange("p g (t m i) -> p g m t i", t=PACK, i=4),
+                in_=raw[:].rearrange("p g (m i t) -> p g m t i", t=PACK, i=4),
+            )
+            return w, sc
+
+        wide, turned, x_grouped, x_codes, x_planes = {}, {}, {}, {}, {}
+        q_ps, p_ps, p_sb, k2_f32, k_grouped, k_codes, k_planes, y_ps = {}, {}, {}, {}, {}, {}, {}, {}
+
+        def widen(i):
+            wide[i] = work.tile([P, N], BF16, name="wide", align_bytes=64)
+            codes = x_raw[i].bitcast(FP8)
+            if i == 0:
+                nc.vector.tensor_copy(out=wide[i][:, : N // 2], in_=codes[:, : N // 2])
+                nc.scalar.copy(out=wide[i][:, N // 2 :], in_=codes[:, N // 2 :])
+            else:
+                nc.scalar.copy(out=wide[i][:], in_=codes)
+
+        def turn(i):
+            turned[i] = psum.tile([P, 2, G, P], F32, name="turned")
+            pairs = wide[i][:].bitcast(F32)
+            for g in range(G):
+                for u in range(2):
+                    nc.tensor.transpose(turned[i][:, u, g, :], pairs[:, 256 * g + u : 256 * (g + 1) : 2], ident[:])
+
+        def scale_x(i):
+            x_grouped[i] = work.tile([P, N], BF16, name="x_grouped", align_bytes=64)
+            halves = turned[i][:].rearrange("p u g n -> p (u g n)").bitcast(BF16)
+            nc.vector.tensor_tensor(
+                out=x_grouped[i][:].rearrange("p (c u e) -> p c u e", u=2, e=2),
+                in0=halves.rearrange("p (u c e) -> p c u e", u=2, e=2),
+                in1=x_sc[:].unsqueeze(2).to_broadcast([P, G, P, PACK]),
+                op=MULT,
+            )
+
+        def quantize_x(i):
+            x_codes[i] = work.tile([P, G * P], I32, name="x_codes", align_bytes=64, bufs=4)
+            x_planes[i] = work.tile([P, G * P], U8, name="x_planes", align_bytes=64, bufs=4)
+            nc.vector.quantize_mx(out=x_codes[i][:].bitcast(FP8X4), scales=x_planes[i][:], in_=x_grouped[i][:])
+
+        def project(i, name, w, sc):
+            acc = psum.tile([P, PACK, P], F32, name=name)
+            for t in range(PACK):
+                cols = slice(P * t, P * (t + 1))
+                for g in range(G):
+                    toks = slice(P * g, P * (g + 1))
+                    nc.tensor.matmul_mx(
+                        out=acc[:, t, :],
+                        lhsT=w[:, g, cols].bitcast(FP8X4),
+                        lhsT_scale=sc[ROWS * g :, cols],
+                        rhs=x_codes[i][:, toks].bitcast(FP8X4),
+                        rhs_scale=x_planes[i][:, toks],
+                        start=(g == 0),
+                        stop=(g == G - 1),
+                    )
+            return acc
+
+        def by_token(acc):
+            return acc[:].rearrange("p t n -> p n t")
+
+        def grouped(flat):
+            return flat.rearrange("p (n t) -> p n t", t=PACK)
+
+        def copy_p(i):
+            p_sb[i] = work.tile([P, R], F32, name="p_sb")
+            nc.scalar.copy(out=grouped(p_sb[i][:]), in_=by_token(p_ps[i]))
+
+        def make_k2(i):
+            k2_f32[i] = work.tile([P, R], F32, name="k2_f32")
+            nc.vector.tensor_tensor(out=grouped(k2_f32[i][:]), in0=by_token(q_ps[i]), in1=grouped(p_sb[i][:]), op=MULT)
+
+        def round_k2(i):
+            k_grouped[i] = work.tile([P, 2 * R], BF16, name="k_grouped", align_bytes=64)
+            nc.scalar.copy(out=k_grouped[i][:, :R], in_=k2_f32[i][:])
+
+        def make_k3(i):
+            if i < TILES - 1:
+                nc.gpsimd.tensor_tensor(out=k_grouped[i][:, R:], in0=p_sb[i][:], in1=k2_f32[i][:], op=MULT)
+            else:
+                nc.vector.tensor_tensor(
+                    out=grouped(k_grouped[i][:, R:]), in0=by_token(p_ps[i]), in1=grouped(k2_f32[i][:]), op=MULT
+                )
+
+        def quantize_k(i):
+            k_codes[i] = work.tile([P, 2 * P], I32, name="k_codes", align_bytes=64)
+            k_planes[i] = work.tile([P, 2 * P], U8, name="k_planes", align_bytes=64)
+            nc.vector.quantize_mx(out=k_codes[i][:].bitcast(FP8X4), scales=k_planes[i][:], in_=k_grouped[i][:])
+
+        def respond_pass(i, j, acc, cols):
+            codes, planes = (x_codes[i], x_planes[i]) if j < G else (k_codes[i], k_planes[i])
+            toks = slice(P * (j % 2), P * (j % 2 + 1))
+            nc.tensor.matmul_mx(
+                out=acc[:],
+                lhsT=codes[:, toks].bitcast(FP8X4),
+                lhsT_scale=planes[:, toks],
+                rhs=h_w[j][:, cols].bitcast(FP8X4),
+                rhs_scale=h_sc[ROWS * j :, cols],
+                start=(j == 0),
+                stop=(j == 3),
+            )
+
+        h_w = [h1_w[:, 0, :], h1_w[:, 1, :], h2_w[:, 0, :], h3_w[:, 0, :]]
+
+        def respond(i):
+            y_ps[i] = psum.tile([P, O], F32, name="y_ps")
+            for j in range(4):
+                respond_pass(i, j, y_ps[i], slice(0, O))
+
+        def store(i, acc, cols, copy):
+            y_sb = work.tile([P, cols.stop - cols.start], F32, name="y_sb", bufs=4)
+            copy(out=y_sb[:], in_=acc[:])
+            nc.sync.dma_start(out=out[P * i : P * (i + 1), cols], in_=y_sb[:])
+
+        whole = slice(0, O)
+        last = TILES - 1
+
+        widen(0)
+        widen(1)
+        turn(0)
+        turn(1)
+        scale_x(0)
+        a_w, a_sc = permute("a", a_raw, a_sc_raw)
+        quantize_x(0)
+        b_w, b_sc = permute("b", b_raw, b_sc_raw)
+        scale_x(1)
+        quantize_x(1)
+        widen(2)
+        for i in range(TILES):
+            p_ps[i] = project(i, "p_ps", a_w, a_sc)
+            if i >= 2 and i % 2 == 0:
+                store(i - 2, y_ps[i - 2], whole, nc.scalar.copy)
+            copy_p(i)
+            q_ps[i] = project(i, "q_ps", b_w, b_sc)
+            if i + 3 < TILES:
+                widen(i + 3)
+            make_k2(i)
+            if i + 2 < TILES:
+                turn(i + 2)
+            round_k2(i)
+            make_k3(i)
+            if i >= 1:
+                respond(i - 1)
+            if i + 2 < TILES:
+                scale_x(i + 2)
+            if i >= 2 and i % 2 == 0:
+                store(i - 1, y_ps[i - 1], whole, nc.vector.tensor_copy)
+            quantize_k(i)
+            if i + 2 < TILES:
+                quantize_x(i + 2)
+        store(last - 1, y_ps[last - 1], whole, nc.scalar.copy)
+        halves = [slice(0, O // 2), slice(O // 2, O)]
+        accs = [psum.tile([P, O // 2], F32, name="turned") for cols in halves]
+        for js in ((0, 1), (2, 3)):
+            for acc, cols in zip(accs, halves):
+                for j in js:
+                    respond_pass(last, j, acc, cols)
+        store(last, accs[0], halves[0], nc.vector.tensor_copy)
+        store(last, accs[1], halves[1], nc.scalar.copy)

@@ -18,6 +18,8 @@ P = 128
 PACK = 4
 G = N // (P * PACK)
 TILES = T // P
+PAIRS = TILES // 2
+W = 2 * P
 QUADS = 4
 ROWS = 4
 
@@ -71,20 +73,21 @@ def tile_factoredcubicvolterraequalizer_w8_kernel(
         h3_w = keep.tile([P, 1, O], I32, name="h3_w", align_bytes=64)
 
         load_x(0, 1)
+        load_x(1, 1)
         nc.sync.dma_start(out=x_sc[:], in_=x_scale.rearrange("o (g p t) -> p (o g) t", p=P, t=PACK))
         load_scales(a_sc_raw, 0, a_scales, nc.sync)
         nc.sync.dma_start(out=a_raw[:], in_=words_view(a_words))
-        load_x(1, 1)
+        load_x(2, 2)
         load_scales(b_sc_raw, 0, b_scales, nc.sync)
         nc.sync.dma_start(out=b_raw[:], in_=words_view(b_words))
-        load_x(2, 2)
+        load_x(4, 2)
         load_scales(h_sc, 0, h1_scales, nc.sync)
+        nc.sync.dma_start(out=h1_w[:], in_=words_view(h1_words))
+        load_x(6, 2)
         load_scales(h_sc, 8, h2_scales, nc.sync)
         load_scales(h_sc, 12, h3_scales, nc.sync)
-        nc.sync.dma_start(out=h1_w[:], in_=words_view(h1_words))
         nc.sync.dma_start(out=h2_w[:], in_=words_view(h2_words))
         nc.sync.dma_start(out=h3_w[:], in_=words_view(h3_words))
-        load_x(4, 4)
 
         def permute(name, raw, sc_raw):
             w = keep.tile([P, G, R], I32, name=name + "_w", align_bytes=64)
@@ -103,7 +106,7 @@ def tile_factoredcubicvolterraequalizer_w8_kernel(
         q_ps, p_ps, p_sb, k2_f32, k_grouped, k_codes, k_planes, y_ps = {}, {}, {}, {}, {}, {}, {}, {}
 
         def widen(i):
-            wide[i] = work.tile([P, N], BF16, name="wide", align_bytes=64)
+            wide[i] = work.tile([P, N], BF16, name="wide", align_bytes=64, bufs=TILES)
             codes = x_raw[i].bitcast(FP8)
             if i == 0:
                 nc.vector.tensor_copy(out=wide[i][:, : N // 2], in_=codes[:, : N // 2])
@@ -119,87 +122,99 @@ def tile_factoredcubicvolterraequalizer_w8_kernel(
                     nc.tensor.transpose(turned[i][:, u, g, :], pairs[:, 256 * g + u : 256 * (g + 1) : 2], ident[:])
 
         def scale_x(i):
-            x_grouped[i] = work.tile([P, N], BF16, name="x_grouped", align_bytes=64)
+            j, side = divmod(i, 2)
+            if side == 0:
+                x_grouped[j] = work.tile([P, G, W * PACK], BF16, name="x_grouped", align_bytes=64)
             halves = turned[i][:].rearrange("p u g n -> p (u g n)").bitcast(BF16)
             nc.vector.tensor_tensor(
-                out=x_grouped[i][:].rearrange("p (c u e) -> p c u e", u=2, e=2),
+                out=x_grouped[j][:, :, P * PACK * side : P * PACK * (side + 1)],
                 in0=halves.rearrange("p (u c e) -> p c u e", u=2, e=2),
                 in1=x_sc[:].unsqueeze(2).to_broadcast([P, G, P, PACK]),
                 op=MULT,
             )
 
-        def quantize_x(i):
-            x_codes[i] = work.tile([P, G * P], I32, name="x_codes", align_bytes=64, bufs=4)
-            x_planes[i] = work.tile([P, G * P], U8, name="x_planes", align_bytes=64, bufs=4)
-            nc.vector.quantize_mx(out=x_codes[i][:].bitcast(FP8X4), scales=x_planes[i][:], in_=x_grouped[i][:])
+        def quantize_x(j):
+            x_codes[j] = work.tile([P, G * W], I32, name="x_codes", align_bytes=64)
+            x_planes[j] = work.tile([P, G * W], U8, name="x_planes", align_bytes=64)
+            nc.vector.quantize_mx(
+                out=x_codes[j][:].bitcast(FP8X4),
+                scales=x_planes[j][:],
+                in_=x_grouped[j][:].rearrange("p g c -> p (g c)"),
+            )
 
-        def project(i, name, w, sc):
-            acc = psum.tile([P, PACK, P], F32, name=name)
-            for t in range(PACK):
-                cols = slice(P * t, P * (t + 1))
-                for g in range(G):
-                    toks = slice(P * g, P * (g + 1))
-                    nc.tensor.matmul_mx(
-                        out=acc[:, t, :],
-                        lhsT=w[:, g, cols].bitcast(FP8X4),
-                        lhsT_scale=sc[ROWS * g :, cols],
-                        rhs=x_codes[i][:, toks].bitcast(FP8X4),
-                        rhs_scale=x_planes[i][:, toks],
-                        start=(g == 0),
-                        stop=(g == G - 1),
-                    )
-            return acc
+        def project(j, name, w, sc):
+            banks = []
+            for h in range(2):
+                acc = psum.tile([P, 2, W], F32, name=name)
+                banks.append(acc)
+                for e in range(2):
+                    t = 2 * h + e
+                    cols = slice(P * t, P * (t + 1))
+                    for g in range(G):
+                        toks = slice(W * g, W * (g + 1))
+                        nc.tensor.matmul_mx(
+                            out=acc[:, e, :],
+                            lhsT=w[:, g, cols].bitcast(FP8X4),
+                            lhsT_scale=sc[ROWS * g :, cols],
+                            rhs=x_codes[j][:, toks].bitcast(FP8X4),
+                            rhs_scale=x_planes[j][:, toks],
+                            start=(g == 0),
+                            stop=(g == G - 1),
+                        )
+            return banks
 
         def by_token(acc):
-            return acc[:].rearrange("p t n -> p n t")
+            return acc[:].rearrange("p e n -> p n e")
 
-        def grouped(flat):
-            return flat.rearrange("p (n t) -> p n t", t=PACK)
+        def copy_p(j):
+            p_sb[j] = work.tile([P, 2, W, 2], F32, name="p_sb", bufs=2)
+            for h in range(2):
+                nc.scalar.copy(out=p_sb[j][:, h], in_=by_token(p_ps[j][h]))
 
-        def copy_p(i):
-            p_sb[i] = work.tile([P, R], F32, name="p_sb")
-            nc.scalar.copy(out=grouped(p_sb[i][:]), in_=by_token(p_ps[i]))
+        def make_k2(j, h):
+            if h == 0:
+                k2_f32[j] = work.tile([P, 2, W, 2], F32, name="k2_f32", bufs=2)
+            nc.vector.tensor_tensor(out=k2_f32[j][:, h], in0=by_token(q_ps[j][h]), in1=p_sb[j][:, h], op=MULT)
 
-        def make_k2(i):
-            k2_f32[i] = work.tile([P, R], F32, name="k2_f32")
-            nc.vector.tensor_tensor(out=grouped(k2_f32[i][:]), in0=by_token(q_ps[i]), in1=grouped(p_sb[i][:]), op=MULT)
+        def joined(src, i):
+            j, side = divmod(i, 2)
+            return src[j][:, :, P * side : P * (side + 1), :].rearrange("p h n e -> p n h e")
 
         def round_k2(i):
-            k_grouped[i] = work.tile([P, 2 * R], BF16, name="k_grouped", align_bytes=64)
-            nc.scalar.copy(out=k_grouped[i][:, :R], in_=k2_f32[i][:])
+            k_grouped[i] = work.tile([P, 2 * R], BF16, name="k_grouped", align_bytes=64, bufs=4)
+            nc.scalar.copy(out=k_grouped[i][:, :R].rearrange("p (n h e) -> p n h e", h=2, e=2), in_=joined(k2_f32, i))
 
-        def make_k3(i):
-            if i < TILES - 1:
-                nc.gpsimd.tensor_tensor(out=k_grouped[i][:, R:], in0=p_sb[i][:], in1=k2_f32[i][:], op=MULT)
-            else:
-                nc.vector.tensor_tensor(
-                    out=grouped(k_grouped[i][:, R:]), in0=by_token(p_ps[i]), in1=grouped(k2_f32[i][:]), op=MULT
-                )
+        def make_k3(i, engine):
+            engine.tensor_tensor(
+                out=k_grouped[i][:, R:].rearrange("p (n h e) -> p n h e", h=2, e=2),
+                in0=joined(p_sb, i),
+                in1=joined(k2_f32, i),
+                op=MULT,
+            )
 
         def quantize_k(i):
-            k_codes[i] = work.tile([P, 2 * P], I32, name="k_codes", align_bytes=64)
-            k_planes[i] = work.tile([P, 2 * P], U8, name="k_planes", align_bytes=64)
+            k_codes[i] = work.tile([P, 2 * P], I32, name="k_codes", align_bytes=64, bufs=4)
+            k_planes[i] = work.tile([P, 2 * P], U8, name="k_planes", align_bytes=64, bufs=4)
             nc.vector.quantize_mx(out=k_codes[i][:].bitcast(FP8X4), scales=k_planes[i][:], in_=k_grouped[i][:])
-
-        def respond_pass(i, j, acc, cols):
-            codes, planes = (x_codes[i], x_planes[i]) if j < G else (k_codes[i], k_planes[i])
-            toks = slice(P * (j % 2), P * (j % 2 + 1))
-            nc.tensor.matmul_mx(
-                out=acc[:],
-                lhsT=codes[:, toks].bitcast(FP8X4),
-                lhsT_scale=planes[:, toks],
-                rhs=h_w[j][:, cols].bitcast(FP8X4),
-                rhs_scale=h_sc[ROWS * j :, cols],
-                start=(j == 0),
-                stop=(j == 3),
-            )
 
         h_w = [h1_w[:, 0, :], h1_w[:, 1, :], h2_w[:, 0, :], h3_w[:, 0, :]]
 
-        def respond(i):
-            y_ps[i] = psum.tile([P, O], F32, name="y_ps")
-            for j in range(4):
-                respond_pass(i, j, y_ps[i], slice(0, O))
+        def respond(i, steps, acc, cols):
+            for s in steps:
+                if s < G:
+                    codes, planes, first = x_codes[i // 2], x_planes[i // 2], W * s + P * (i % 2)
+                else:
+                    codes, planes, first = k_codes[i], k_planes[i], P * (s - G)
+                toks = slice(first, first + P)
+                nc.tensor.matmul_mx(
+                    out=acc[:],
+                    lhsT=codes[:, toks].bitcast(FP8X4),
+                    lhsT_scale=planes[:, toks],
+                    rhs=h_w[s][:, cols].bitcast(FP8X4),
+                    rhs_scale=h_sc[ROWS * s :, cols],
+                    start=(s == 0),
+                    stop=(s == 3),
+                )
 
         def store(i, acc, cols, copy):
             y_sb = work.tile([P, cols.stop - cols.start], F32, name="y_sb", bufs=4)
@@ -209,45 +224,69 @@ def tile_factoredcubicvolterraequalizer_w8_kernel(
         whole = slice(0, O)
         last = TILES - 1
 
+        halves = [slice(0, O // 2), slice(O // 2, O)]
+        linear, higher = (0, 1), (2, 3)
+
         widen(0)
         widen(1)
         turn(0)
         turn(1)
         scale_x(0)
+        widen(2)
+        turn(2)
+        scale_x(1)
+        widen(3)
+        turn(3)
         a_w, a_sc = permute("a", a_raw, a_sc_raw)
         quantize_x(0)
+        widen(4)
+        widen(5)
         b_w, b_sc = permute("b", b_raw, b_sc_raw)
-        scale_x(1)
-        quantize_x(1)
-        widen(2)
-        for i in range(TILES):
-            p_ps[i] = project(i, "p_ps", a_w, a_sc)
-            if i >= 2 and i % 2 == 0:
-                store(i - 2, y_ps[i - 2], whole, nc.scalar.copy)
-            copy_p(i)
-            q_ps[i] = project(i, "q_ps", b_w, b_sc)
-            if i + 3 < TILES:
-                widen(i + 3)
-            make_k2(i)
-            if i + 2 < TILES:
-                turn(i + 2)
-            round_k2(i)
-            make_k3(i)
-            if i >= 1:
-                respond(i - 1)
-            if i + 2 < TILES:
-                scale_x(i + 2)
-            if i >= 2 and i % 2 == 0:
-                store(i - 1, y_ps[i - 1], whole, nc.vector.tensor_copy)
-            quantize_k(i)
-            if i + 2 < TILES:
-                quantize_x(i + 2)
+        scale_x(2)
+        scale_x(3)
+        for j in range(PAIRS):
+            first, second = 2 * j, 2 * j + 1
+            p_ps[j] = project(j, "p_ps", a_w, a_sc)
+            copy_p(j)
+            if j + 3 < PAIRS:
+                widen(first + 6)
+                widen(second + 6)
+            q_ps[j] = project(j, "q_ps", b_w, b_sc)
+            make_k2(j, 0)
+            if j + 1 < PAIRS:
+                quantize_x(j + 1)
+            make_k2(j, 1)
+            if j + 2 < PAIRS:
+                turn(first + 4)
+                turn(second + 4)
+            if j >= 1:
+                for i in (first - 2, second - 2):
+                    respond(i, higher, y_ps[i], whole)
+                    store(i, y_ps[i], whole, nc.scalar.copy)
+            for i in (first, second):
+                if i < last:
+                    y_ps[i] = psum.tile([P, O], F32, name="turned" if j == 2 else "y_ps")
+                    respond(i, linear, y_ps[i], whole)
+                else:
+                    left = psum.tile([P, O // 2], F32, name="y_ps")
+                    right = psum.tile([P, O // 2], F32, name="p_ps")
+                    respond(i, linear, left, halves[0])
+                    respond(i, linear, right, halves[1])
+            round_k2(first)
+            round_k2(second)
+            if j + 2 < PAIRS:
+                make_k3(first, nc.gpsimd)
+                make_k3(second, nc.gpsimd)
+                scale_x(first + 4)
+                scale_x(second + 4)
+            else:
+                make_k3(first, nc.vector)
+                make_k3(second, nc.vector)
+            quantize_k(first)
+            quantize_k(second)
+        respond(last - 1, higher, y_ps[last - 1], whole)
         store(last - 1, y_ps[last - 1], whole, nc.scalar.copy)
-        halves = [slice(0, O // 2), slice(O // 2, O)]
-        accs = [psum.tile([P, O // 2], F32, name="turned") for cols in halves]
-        for js in ((0, 1), (2, 3)):
-            for acc, cols in zip(accs, halves):
-                for j in js:
-                    respond_pass(last, j, acc, cols)
-        store(last, accs[0], halves[0], nc.vector.tensor_copy)
-        store(last, accs[1], halves[1], nc.scalar.copy)
+        respond(last, higher, left, halves[0])
+        respond(last, higher, right, halves[1])
+        store(last, left, halves[0], nc.vector.tensor_copy)
+        store(last, right, halves[1], nc.scalar.copy)

@@ -53,7 +53,8 @@ def tile_factoredcubicvolterraequalizer_w8_kernel(
         b_sc_raw = keep.tile([P, R], U8, name="b_sc_raw", align_bytes=64)
         a_sc_raw = keep.tile([P, R], U8, name="a_sc_raw", align_bytes=64)
         h_sc = keep.tile([P, O], U8, name="h_sc", align_bytes=64)
-        for plane in (a_sc_raw, b_sc_raw, h_sc):
+        h1_sc = keep.tile([P, O], U8, name="h1_sc", align_bytes=64)
+        for plane in (a_sc_raw, b_sc_raw, h1_sc, h_sc):
             nc.vector.memset(plane[:].bitcast(I32), 0)
 
         x_raw = {}
@@ -75,24 +76,24 @@ def tile_factoredcubicvolterraequalizer_w8_kernel(
         load_x(0, 1)
         load_x(1, 1)
         nc.sync.dma_start(out=x_sc[:], in_=x_scale.rearrange("o (g p t) -> p (o g) t", p=P, t=PACK))
-        load_scales(a_sc_raw, 0, a_scales, nc.sync)
-        nc.sync.dma_start(out=a_raw[:], in_=words_view(a_words))
         load_x(2, 2)
-        load_scales(b_sc_raw, 0, b_scales, nc.sync)
+        nc.sync.dma_start(out=a_raw[:], in_=words_view(a_words))
+        load_scales(a_sc_raw, 0, a_scales, nc.sync)
         nc.sync.dma_start(out=b_raw[:], in_=words_view(b_words))
+        load_scales(b_sc_raw, 0, b_scales, nc.sync)
         load_x(4, 2)
-        load_scales(h_sc, 0, h1_scales, nc.sync)
         nc.sync.dma_start(out=h1_w[:], in_=words_view(h1_words))
+        load_scales(h1_sc, 0, h1_scales, nc.sync)
         load_x(6, 2)
-        load_scales(h_sc, 8, h2_scales, nc.sync)
-        load_scales(h_sc, 12, h3_scales, nc.sync)
         nc.sync.dma_start(out=h2_w[:], in_=words_view(h2_words))
         nc.sync.dma_start(out=h3_w[:], in_=words_view(h3_words))
+        load_scales(h_sc, 0, h2_scales, nc.sync)
+        load_scales(h_sc, 4, h3_scales, nc.sync)
 
         def permute(name, raw, sc_raw):
             w = keep.tile([P, G, R], I32, name=name + "_w", align_bytes=64)
             sc = keep.tile([P, R], U8, name=name + "_sc", align_bytes=64)
-            nc.vector.tensor_copy(
+            nc.gpsimd.tensor_copy(
                 out=sc[:].rearrange("p (t m) -> p t m", t=PACK),
                 in_=sc_raw[:].rearrange("p (m t) -> p t m", t=PACK),
             )
@@ -111,25 +112,33 @@ def tile_factoredcubicvolterraequalizer_w8_kernel(
             if i == 0:
                 nc.vector.tensor_copy(out=wide[i][:, : N // 2], in_=codes[:, : N // 2])
                 nc.scalar.copy(out=wide[i][:, N // 2 :], in_=codes[:, N // 2 :])
+            elif i == 1:
+                nc.scalar.copy(out=wide[i][:, : N // 2], in_=codes[:, : N // 2])
+                nc.gpsimd.tensor_copy(out=wide[i][:, N // 2 :], in_=codes[:, N // 2 :])
             else:
                 nc.scalar.copy(out=wide[i][:], in_=codes)
 
-        def turn(i):
-            turned[i] = psum.tile([P, 2, G, P], F32, name="turned")
+        def turn(i, groups=slice(0, G), name="turned"):
+            count = groups.stop - groups.start
+            bank = psum.tile([P, 2, count, P], F32, name=name)
+            turned[i, groups.start] = bank
             pairs = wide[i][:].bitcast(F32)
-            for g in range(G):
+            for g in range(groups.start, groups.stop):
                 for u in range(2):
-                    nc.tensor.transpose(turned[i][:, u, g, :], pairs[:, 256 * g + u : 256 * (g + 1) : 2], ident[:])
+                    nc.tensor.transpose(
+                        bank[:, u, g - groups.start, :], pairs[:, 256 * g + u : 256 * (g + 1) : 2], ident[:]
+                    )
 
-        def scale_x(i):
+        def scale_x(i, groups=slice(0, G)):
             j, side = divmod(i, 2)
-            if side == 0:
+            count = groups.stop - groups.start
+            if j not in x_grouped:
                 x_grouped[j] = work.tile([P, G, W * PACK], BF16, name="x_grouped", align_bytes=64)
-            halves = turned[i][:].rearrange("p u g n -> p (u g n)").bitcast(BF16)
+            halves = turned[i, groups.start][:].rearrange("p u g n -> p (u g n)").bitcast(BF16)
             nc.vector.tensor_tensor(
-                out=x_grouped[j][:, :, P * PACK * side : P * PACK * (side + 1)],
+                out=x_grouped[j][:, groups, P * PACK * side : P * PACK * (side + 1)],
                 in0=halves.rearrange("p (u c e) -> p c u e", u=2, e=2),
-                in1=x_sc[:].unsqueeze(2).to_broadcast([P, G, P, PACK]),
+                in1=x_sc[:, groups, :].unsqueeze(2).to_broadcast([P, count, P, PACK]),
                 op=MULT,
             )
 
@@ -211,13 +220,13 @@ def tile_factoredcubicvolterraequalizer_w8_kernel(
                     lhsT=codes[:, toks].bitcast(FP8X4),
                     lhsT_scale=planes[:, toks],
                     rhs=h_w[s][:, cols].bitcast(FP8X4),
-                    rhs_scale=h_sc[ROWS * s :, cols],
+                    rhs_scale=(h1_sc if s < G else h_sc)[ROWS * (s % 2) :, cols],
                     start=(s == 0),
                     stop=(s == 3),
                 )
 
         def store(i, acc, cols, copy):
-            y_sb = work.tile([P, cols.stop - cols.start], F32, name="y_sb", bufs=4)
+            y_sb = work.tile([P, cols.stop - cols.start], F32, name="y_sb", bufs=6)
             copy(out=y_sb[:], in_=acc[:])
             nc.sync.dma_start(out=out[P * i : P * (i + 1), cols], in_=y_sb[:])
 
@@ -227,13 +236,24 @@ def tile_factoredcubicvolterraequalizer_w8_kernel(
         halves = [slice(0, O // 2), slice(O // 2, O)]
         linear, higher = (0, 1), (2, 3)
 
+        idle = psum.tile([P, P], F32, name="y_ps")
+
+        def warm(count):
+            for c in range(count):
+                nc.tensor.matmul(idle[:], lhsT=ident[:], rhs=ident[:], start=True, stop=True)
+
+        warm(3)
         widen(0)
         widen(1)
-        turn(0)
+        turn(0, slice(0, 1), "p_ps")
+        turn(0, slice(1, 2))
         turn(1)
-        scale_x(0)
+        warm(2)
+        scale_x(0, slice(0, 1))
+        scale_x(0, slice(1, 2))
         widen(2)
         turn(2)
+        warm(2)
         scale_x(1)
         widen(3)
         turn(3)
@@ -262,31 +282,31 @@ def tile_factoredcubicvolterraequalizer_w8_kernel(
             if j >= 1:
                 for i in (first - 2, second - 2):
                     respond(i, higher, y_ps[i], whole)
-                    store(i, y_ps[i], whole, nc.scalar.copy)
+                    if i != last - 2:
+                        store(i, y_ps[i], whole, nc.scalar.copy)
             for i in (first, second):
-                if i < last:
+                if j + 1 < PAIRS:
                     y_ps[i] = psum.tile([P, O], F32, name="turned" if j == 2 else "y_ps")
                     respond(i, linear, y_ps[i], whole)
                 else:
-                    left = psum.tile([P, O // 2], F32, name="y_ps")
-                    right = psum.tile([P, O // 2], F32, name="p_ps")
-                    respond(i, linear, left, halves[0])
-                    respond(i, linear, right, halves[1])
+                    for cols, name in zip(halves, ("y_ps", "p_ps")):
+                        y_ps[i, cols.start] = psum.tile([P, O // 2], F32, name=name)
+                        respond(i, linear, y_ps[i, cols.start], cols)
             round_k2(first)
             round_k2(second)
+            if second == last:
+                store(last - 2, y_ps[last - 2], whole, nc.scalar.copy)
             if j + 2 < PAIRS:
                 make_k3(first, nc.gpsimd)
-                make_k3(second, nc.gpsimd)
                 scale_x(first + 4)
                 scale_x(second + 4)
+                make_k3(second, nc.vector)
             else:
                 make_k3(first, nc.vector)
                 make_k3(second, nc.vector)
             quantize_k(first)
             quantize_k(second)
-        respond(last - 1, higher, y_ps[last - 1], whole)
-        store(last - 1, y_ps[last - 1], whole, nc.scalar.copy)
-        respond(last, higher, left, halves[0])
-        respond(last, higher, right, halves[1])
-        store(last, left, halves[0], nc.vector.tensor_copy)
-        store(last, right, halves[1], nc.scalar.copy)
+        for i in (last - 1, last):
+            for cols, copy in zip(halves, (nc.scalar.copy, nc.vector.tensor_copy)):
+                respond(i, higher, y_ps[i, cols.start], cols)
+                store(i, y_ps[i, cols.start], cols, copy)

@@ -35,8 +35,6 @@ def tile_factoredcubicvolterraequalizer_w8_kernel(
         psum = ctx.enter_context(tc.psum_pool(name="psum", bufs=2))
         ctx.enter_context(tc.manual_schedule())
 
-        ident = keep.tile([P, P], F32, name="ident")
-        make_identity(nc, ident[:])
 
         def words_view(words):
             return words.rearrange("g p n t -> p g (n t)").bitcast(I32)
@@ -54,8 +52,13 @@ def tile_factoredcubicvolterraequalizer_w8_kernel(
         a_sc_raw = keep.tile([P, R], U8, name="a_sc_raw", align_bytes=64)
         h_sc = keep.tile([P, O], U8, name="h_sc", align_bytes=64)
         h1_sc = keep.tile([P, O], U8, name="h1_sc", align_bytes=64)
-        for plane in (a_sc_raw, b_sc_raw, h1_sc, h_sc):
+        for plane in (a_sc_raw, b_sc_raw):
+            nc.gpsimd.memset(plane[:].bitcast(I32), 0)
+        for plane in (h1_sc, h_sc):
             nc.vector.memset(plane[:].bitcast(I32), 0)
+
+        ident = keep.tile([P, P], F32, name="ident")
+        make_identity(nc, ident[:])
 
         x_raw = {}
 
@@ -74,13 +77,13 @@ def tile_factoredcubicvolterraequalizer_w8_kernel(
         h3_w = keep.tile([P, 1, O], I32, name="h3_w", align_bytes=64)
 
         load_x(0, 1)
+        load_scales(a_sc_raw, 0, a_scales, nc.sync)
         load_x(1, 1)
         nc.sync.dma_start(out=x_sc[:], in_=x_scale.rearrange("o (g p t) -> p (o g) t", p=P, t=PACK))
         load_x(2, 2)
-        nc.sync.dma_start(out=a_raw[:], in_=words_view(a_words))
-        load_scales(a_sc_raw, 0, a_scales, nc.sync)
-        nc.sync.dma_start(out=b_raw[:], in_=words_view(b_words))
         load_scales(b_sc_raw, 0, b_scales, nc.sync)
+        nc.sync.dma_start(out=a_raw[:], in_=words_view(a_words))
+        nc.sync.dma_start(out=b_raw[:], in_=words_view(b_words))
         load_x(4, 2)
         nc.sync.dma_start(out=h1_w[:], in_=words_view(h1_words))
         load_scales(h1_sc, 0, h1_scales, nc.sync)
@@ -90,18 +93,21 @@ def tile_factoredcubicvolterraequalizer_w8_kernel(
         load_scales(h_sc, 0, h2_scales, nc.sync)
         load_scales(h_sc, 4, h3_scales, nc.sync)
 
-        def permute(name, raw, sc_raw):
-            w = keep.tile([P, G, R], I32, name=name + "_w", align_bytes=64)
-            sc = keep.tile([P, R], U8, name=name + "_sc", align_bytes=64)
-            nc.gpsimd.tensor_copy(
+        def permute_scales(name, sc_raw, engine):
+            sc = keep.tile([P, R], U8, name=name, align_bytes=64)
+            engine.tensor_copy(
                 out=sc[:].rearrange("p (t m) -> p t m", t=PACK),
                 in_=sc_raw[:].rearrange("p (m t) -> p t m", t=PACK),
             )
+            return sc
+
+        def permute_words(name, raw):
+            w = keep.tile([P, G, R], I32, name=name, align_bytes=64)
             nc.vector.tensor_copy(
                 out=w[:].rearrange("p g (t m i) -> p g m t i", t=PACK, i=4),
                 in_=raw[:].rearrange("p g (m i t) -> p g m t i", t=PACK, i=4),
             )
-            return w, sc
+            return w
 
         wide, turned, x_grouped, x_codes, x_planes = {}, {}, {}, {}, {}
         q_ps, p_ps, p_sb, k2_f32, k_grouped, k_codes, k_planes, y_ps = {}, {}, {}, {}, {}, {}, {}, {}
@@ -109,12 +115,9 @@ def tile_factoredcubicvolterraequalizer_w8_kernel(
         def widen(i):
             wide[i] = work.tile([P, N], BF16, name="wide", align_bytes=64, bufs=TILES)
             codes = x_raw[i].bitcast(FP8)
-            if i == 0:
+            if i < 2:
                 nc.vector.tensor_copy(out=wide[i][:, : N // 2], in_=codes[:, : N // 2])
                 nc.scalar.copy(out=wide[i][:, N // 2 :], in_=codes[:, N // 2 :])
-            elif i == 1:
-                nc.scalar.copy(out=wide[i][:, : N // 2], in_=codes[:, : N // 2])
-                nc.gpsimd.tensor_copy(out=wide[i][:, N // 2 :], in_=codes[:, N // 2 :])
             else:
                 nc.scalar.copy(out=wide[i][:], in_=codes)
 
@@ -180,10 +183,12 @@ def tile_factoredcubicvolterraequalizer_w8_kernel(
             for h in range(2):
                 nc.scalar.copy(out=p_sb[j][:, h], in_=by_token(p_ps[j][h]))
 
-        def make_k2(j, h):
+        def make_k2(j, h, toks=slice(0, W)):
             if h == 0:
                 k2_f32[j] = work.tile([P, 2, W, 2], F32, name="k2_f32", bufs=2)
-            nc.vector.tensor_tensor(out=k2_f32[j][:, h], in0=by_token(q_ps[j][h]), in1=p_sb[j][:, h], op=MULT)
+            nc.vector.tensor_tensor(
+                out=k2_f32[j][:, h, toks], in0=by_token(q_ps[j][h])[:, toks], in1=p_sb[j][:, h, toks], op=MULT
+            )
 
         def joined(src, i):
             j, side = divmod(i, 2)
@@ -245,6 +250,8 @@ def tile_factoredcubicvolterraequalizer_w8_kernel(
         warm(3)
         widen(0)
         widen(1)
+        a_sc = permute_scales("a_sc", a_sc_raw, nc.vector)
+        b_sc = permute_scales("b_sc", b_sc_raw, nc.gpsimd)
         turn(0, slice(0, 1), "p_ps")
         turn(0, slice(1, 2))
         turn(1)
@@ -257,11 +264,11 @@ def tile_factoredcubicvolterraequalizer_w8_kernel(
         scale_x(1)
         widen(3)
         turn(3)
-        a_w, a_sc = permute("a", a_raw, a_sc_raw)
+        a_w = permute_words("a_w", a_raw)
         quantize_x(0)
         widen(4)
         widen(5)
-        b_w, b_sc = permute("b", b_raw, b_sc_raw)
+        b_w = permute_words("b_w", b_raw)
         scale_x(2)
         scale_x(3)
         for j in range(PAIRS):
@@ -275,10 +282,13 @@ def tile_factoredcubicvolterraequalizer_w8_kernel(
             make_k2(j, 0)
             if j + 1 < PAIRS:
                 quantize_x(j + 1)
-            make_k2(j, 1)
             if j + 2 < PAIRS:
+                make_k2(j, 1)
                 turn(first + 4)
                 turn(second + 4)
+            else:
+                make_k2(j, 1, slice(0, P))
+                make_k2(j, 1, slice(P, W))
             if j >= 1:
                 for i in (first - 2, second - 2):
                     respond(i, higher, y_ps[i], whole)

@@ -308,9 +308,9 @@ def tile_factoredcubicvolterraequalizer_w8_kernel(
                 store(last - 2, y_ps[last - 2], whole, nc.scalar.copy)
             if j + 2 < PAIRS:
                 make_k3(first, nc.gpsimd)
+                make_k3(second, nc.gpsimd)
                 scale_x(first + 4)
                 scale_x(second + 4)
-                make_k3(second, nc.vector)
             else:
                 make_k3(first, nc.vector)
                 make_k3(second, nc.vector)

from contextlib import ExitStack

import concourse.mybir as mybir
from concourse.masks import make_identity

T, N, R, O = 1024, 1024, 512, 512
FLOPS = 2 * T * (2 * N * R + N * O + 2 * R * O)

F32 = mybir.dt.float32
BF16 = mybir.dt.bfloat16
I32 = mybir.dt.int32
U8 = mybir.dt.uint8
FP8 = mybir.dt.float8_e4m3fn
FP8X4 = mybir.dt.float8_e4m3fn_x4
MULT = mybir.AluOpType.mult

P = 128
PACK = 4
G = N // (P * PACK)
TILES = T // P
PAIRS = TILES // 2
W = 2 * P
QUADS = 4
ROWS = 4


def tile_factoredcubicvolterraequalizer_w8_kernel(
    tc, x_bytes, x_scale, a_words, a_scales, b_words, b_scales, h1_words, h1_scales,
    h2_words, h2_scales, h3_words, h3_scales, out
):
    nc = tc.nc
    with ExitStack() as ctx:
        keep = ctx.enter_context(tc.tile_pool(name="keep", bufs=1))
        work = ctx.enter_context(tc.tile_pool(name="work", bufs=3))
        psum = ctx.enter_context(tc.psum_pool(name="psum", bufs=2))
        ctx.enter_context(tc.manual_schedule())


        def words_view(words):
            return words.rearrange("g p n t -> p g (n t)").bitcast(I32)

        def load_scales(plane, first_row, scales, queue):
            groups = scales.shape[0]
            for quad in range(QUADS):
                lo = 32 * quad + first_row
                queue.dma_start(
                    out=plane[lo : lo + ROWS * groups, :].bitcast(I32),
                    in_=scales[:, ROWS * quad : ROWS * (quad + 1), :].bitcast(I32),
                )

        b_sc_raw = keep.tile([P, R], U8, name="b_sc_raw", align_bytes=64)
        a_sc_raw = keep.tile([P, R], U8, name="a_sc_raw", align_bytes=64)
        h_sc = keep.tile([P, O], U8, name="h_sc", align_bytes=64)
        h1_sc = keep.tile([P, O], U8, name="h1_sc", align_bytes=64)
        for plane in (a_sc_raw, b_sc_raw):
            nc.gpsimd.memset(plane[:].bitcast(I32), 0)
        for plane in (h1_sc, h_sc):
            nc.vector.memset(plane[:].bitcast(I32), 0)

        ident = keep.tile([P, P], F32, name="ident")
        make_identity(nc, ident[:])

        x_raw = {}

        def load_x(first, count):
            xbytes = keep.tile([P, count, N], U8, name="xbytes%d" % first, align_bytes=64)
            rows = x_bytes[first * P : (first + count) * P, :]
            nc.sync.dma_start(out=xbytes[:], in_=rows.rearrange("(j p) k -> p j k", p=P))
            for j in range(count):
                x_raw[first + j] = xbytes[:, j, :]

        x_sc = keep.tile([P, G, PACK], F32, name="x_sc")
        b_raw = keep.tile([P, G, R], I32, name="b_raw", align_bytes=64)
        a_raw = keep.tile([P, G, R], I32, name="a_raw", align_bytes=64)
        h1_w = keep.tile([P, G, O], I32, name="h1_w", align_bytes=64)
        h2_w = keep.tile([P, 1, O], I32, name="h2_w", align_bytes=64)
        h3_w = keep.tile([P, 1, O], I32, name="h3_w", align_bytes=64)

        load_x(0, 1)
        load_scales(a_sc_raw, 0, a_scales, nc.sync)
        load_x(1, 1)
        nc.sync.dma_start(out=x_sc[:], in_=x_scale.rearrange("o (g p t) -> p (o g) t", p=P, t=PACK))
        load_x(2, 2)
        load_scales(b_sc_raw, 0, b_scales, nc.sync)
        nc.sync.dma_start(out=a_raw[:], in_=words_view(a_words))
        nc.sync.dma_start(out=b_raw[:], in_=words_view(b_words))
        load_x(4, 2)
        nc.sync.dma_start(out=h1_w[:], in_=words_view(h1_words))
        load_scales(h1_sc, 0, h1_scales, nc.sync)
        load_x(6, 2)
        nc.sync.dma_start(out=h2_w[:], in_=words_view(h2_words))
        nc.sync.dma_start(out=h3_w[:], in_=words_view(h3_words))
        load_scales(h_sc, 0, h2_scales, nc.sync)
        load_scales(h_sc, 4, h3_scales, nc.sync)

        def permute_scales(name, sc_raw, engine):
            sc = keep.tile([P, R], U8, name=name, align_bytes=64)
            engine.tensor_copy(
                out=sc[:].rearrange("p (t m) -> p t m", t=PACK),
                in_=sc_raw[:].rearrange("p (m t) -> p t m", t=PACK),
            )
            return sc

        def permute_words(name, raw):
            w = keep.tile([P, G, R], I32, name=name, align_bytes=64)
            nc.vector.tensor_copy(
                out=w[:].rearrange("p g (t m i) -> p g m t i", t=PACK, i=4),
                in_=raw[:].rearrange("p g (m i t) -> p g m t i", t=PACK, i=4),
            )
            return w

        wide, turned, x_grouped, x_codes, x_planes = {}, {}, {}, {}, {}
        q_ps, p_ps, p_sb, k2_f32, k_grouped, k_codes, k_planes, y_ps = {}, {}, {}, {}, {}, {}, {}, {}

        def widen(i):
            wide[i] = work.tile([P, N], BF16, name="wide", align_bytes=64, bufs=TILES)
            codes = x_raw[i].bitcast(FP8)
            if i < 2:
                nc.vector.tensor_copy(out=wide[i][:, : N // 2], in_=codes[:, : N // 2])
                nc.scalar.copy(out=wide[i][:, N // 2 :], in_=codes[:, N // 2 :])
            else:
                nc.scalar.copy(out=wide[i][:], in_=codes)

        def turn(i, groups=slice(0, G), name="turned"):
            count = groups.stop - groups.start
            bank = psum.tile([P, 2, count, P], F32, name=name)
            turned[i, groups.start] = bank
            pairs = wide[i][:].bitcast(F32)
            for g in range(groups.start, groups.stop):
                for u in range(2):
                    nc.tensor.transpose(
                        bank[:, u, g - groups.start, :], pairs[:, 256 * g + u : 256 * (g + 1) : 2], ident[:]
                    )

        def scale_x(i, groups=slice(0, G)):
            j, side = divmod(i, 2)
            count = groups.stop - groups.start
            if j not in x_grouped:
                x_grouped[j] = work.tile([P, G, W * PACK], BF16, name="x_grouped", align_bytes=64)
            halves = turned[i, groups.start][:].rearrange("p u g n -> p (u g n)").bitcast(BF16)
            nc.vector.tensor_tensor(
                out=x_grouped[j][:, groups, P * PACK * side : P * PACK * (side + 1)],
                in0=halves.rearrange("p (u c e) -> p c u e", u=2, e=2),
                in1=x_sc[:, groups, :].unsqueeze(2).to_broadcast([P, count, P, PACK]),
                op=MULT,
            )

        def quantize_x(j):
            x_codes[j] = work.tile([P, G * W], I32, name="x_codes", align_bytes=64)
            x_planes[j] = work.tile([P, G * W], U8, name="x_planes", align_bytes=64)
            nc.vector.quantize_mx(
                out=x_codes[j][:].bitcast(FP8X4),
                scales=x_planes[j][:],
                in_=x_grouped[j][:].rearrange("p g c -> p (g c)"),
            )

        def project(j, name, w, sc):
            banks = []
            for h in range(2):
                acc = psum.tile([P, 2, W], F32, name=name)
                banks.append(acc)
                for e in range(2):
                    t = 2 * h + e
                    cols = slice(P * t, P * (t + 1))
                    for g in range(G):
                        toks = slice(W * g, W * (g + 1))
                        nc.tensor.matmul_mx(
                            out=acc[:, e, :],
                            lhsT=w[:, g, cols].bitcast(FP8X4),
                            lhsT_scale=sc[ROWS * g :, cols],
                            rhs=x_codes[j][:, toks].bitcast(FP8X4),
                            rhs_scale=x_planes[j][:, toks],
                            start=(g == 0),
                            stop=(g == G - 1),
                        )
            return banks

        def by_token(acc):
            return acc[:].rearrange("p e n -> p n e")

        def copy_p(j):
            p_sb[j] = work.tile([P, 2, W, 2], F32, name="p_sb", bufs=2)
            for h in range(2):
                nc.scalar.copy(out=p_sb[j][:, h], in_=by_token(p_ps[j][h]))

        def make_k2(j, h, toks=slice(0, W)):
            if h == 0:
                k2_f32[j] = work.tile([P, 2, W, 2], F32, name="k2_f32", bufs=2)
            nc.vector.tensor_tensor(
                out=k2_f32[j][:, h, toks], in0=by_token(q_ps[j][h])[:, toks], in1=p_sb[j][:, h, toks], op=MULT
            )

        def joined(src, i):
            j, side = divmod(i, 2)
            return src[j][:, :, P * side : P * (side + 1), :].rearrange("p h n e -> p n h e")

        def round_k2(i):
            k_grouped[i] = work.tile([P, 2 * R], BF16, name="k_grouped", align_bytes=64, bufs=4)
            nc.scalar.copy(out=k_grouped[i][:, :R].rearrange("p (n h e) -> p n h e", h=2, e=2), in_=joined(k2_f32, i))

        def make_k3(i, engine):
            engine.tensor_tensor(
                out=k_grouped[i][:, R:].rearrange("p (n h e) -> p n h e", h=2, e=2),
                in0=joined(p_sb, i),
                in1=joined(k2_f32, i),
                op=MULT,
            )

        def quantize_k(i):
            k_codes[i] = work.tile([P, 2 * P], I32, name="k_codes", align_bytes=64, bufs=4)
            k_planes[i] = work.tile([P, 2 * P], U8, name="k_planes", align_bytes=64, bufs=4)
            nc.vector.quantize_mx(out=k_codes[i][:].bitcast(FP8X4), scales=k_planes[i][:], in_=k_grouped[i][:])

        h_w = [h1_w[:, 0, :], h1_w[:, 1, :], h2_w[:, 0, :], h3_w[:, 0, :]]

        def respond(i, steps, acc, cols):
            for s in steps:
                if s < G:
                    codes, planes, first = x_codes[i // 2], x_planes[i // 2], W * s + P * (i % 2)
                else:
                    codes, planes, first = k_codes[i], k_planes[i], P * (s - G)
                toks = slice(first, first + P)
                nc.tensor.matmul_mx(
                    out=acc[:],
                    lhsT=codes[:, toks].bitcast(FP8X4),
                    lhsT_scale=planes[:, toks],
                    rhs=h_w[s][:, cols].bitcast(FP8X4),
                    rhs_scale=(h1_sc if s < G else h_sc)[ROWS * (s % 2) :, cols],
                    start=(s == 0),
                    stop=(s == 3),
                )

        def store(i, acc, cols, copy):
            y_sb = work.tile([P, cols.stop - cols.start], F32, name="y_sb", bufs=6)
            copy(out=y_sb[:], in_=acc[:])
            nc.sync.dma_start(out=out[P * i : P * (i + 1), cols], in_=y_sb[:])

        whole = slice(0, O)
        last = TILES - 1

        halves = [slice(0, O // 2), slice(O // 2, O)]
        linear, higher = (0, 1), (2, 3)

        idle = psum.tile([P, P], F32, name="y_ps")

        def warm(count):
            for c in range(count):
                nc.tensor.matmul(idle[:], lhsT=ident[:], rhs=ident[:], start=True, stop=True)

        warm(3)
        widen(0)
        widen(1)
        a_sc = permute_scales("a_sc", a_sc_raw, nc.vector)
        b_sc = permute_scales("b_sc", b_sc_raw, nc.gpsimd)
        turn(0, slice(0, 1), "p_ps")
        turn(0, slice(1, 2))
        turn(1)
        warm(2)
        scale_x(0, slice(0, 1))
        scale_x(0, slice(1, 2))
        widen(2)
        turn(2)
        warm(2)
        scale_x(1)
        widen(3)
        turn(3)
        a_w = permute_words("a_w", a_raw)
        quantize_x(0)
        widen(4)
        widen(5)
        b_w = permute_words("b_w", b_raw)
        scale_x(2)
        scale_x(3)
        for j in range(PAIRS):
            first, second = 2 * j, 2 * j + 1
            p_ps[j] = project(j, "p_ps", a_w, a_sc)
            copy_p(j)
            if j + 3 < PAIRS:
                widen(first + 6)
                widen(second + 6)
            q_ps[j] = project(j, "q_ps", b_w, b_sc)
            make_k2(j, 0)
            if j + 1 < PAIRS:
                quantize_x(j + 1)
            if j + 2 < PAIRS:
                make_k2(j, 1)
                turn(first + 4)
                turn(second + 4)
            else:
                make_k2(j, 1, slice(0, P))
                make_k2(j, 1, slice(P, W))
            if j >= 1:
                for i in (first - 2, second - 2):
                    respond(i, higher, y_ps[i], whole)
                    if i != last - 2:
                        store(i, y_ps[i], whole, nc.scalar.copy)
            for i in (first, second):
                if j + 1 < PAIRS:
                    y_ps[i] = psum.tile([P, O], F32, name="turned" if j == 2 else "y_ps")
                    respond(i, linear, y_ps[i], whole)
                else:
                    for cols, name in zip(halves, ("y_ps", "p_ps")):
                        y_ps[i, cols.start] = psum.tile([P, O // 2], F32, name=name)
                        respond(i, linear, y_ps[i, cols.start], cols)
            round_k2(first)
            round_k2(second)
            if second == last:
                store(last - 2, y_ps[last - 2], whole, nc.scalar.copy)
            if j + 2 < PAIRS:
                make_k3(first, nc.gpsimd)
                make_k3(second, nc.gpsimd)
                scale_x(first + 4)
                scale_x(second + 4)
            else:
                make_k3(first, nc.vector)
                make_k3(second, nc.vector)
            quantize_k(first)
            quantize_k(second)
        for i in (last - 1, last):
            for cols, copy in zip(halves, (nc.scalar.copy, nc.vector.tensor_copy)):
                respond(i, higher, y_ps[i, cols.start], cols)
                store(i, y_ps[i, cols.start], cols, copy)
